import numpy as np
import ml_dtypes


def mxq(x, axis, fmt="e4m3"):
    dtype, down = {"e4m3": (ml_dtypes.float8_e4m3fn, 7), "e5m2": (ml_dtypes.float8_e5m2, 14)}[fmt]
    v = np.moveaxis(np.asarray(x, np.float32).astype(ml_dtypes.bfloat16).astype(np.float64), axis, -1)
    blocks = v.reshape(v.shape[:-1] + (-1, 32))
    amax = np.abs(blocks).max(-1, keepdims=True)
    byte = np.maximum(np.where(amax > 0, np.frexp(amax)[1] - 1 + 127, 0) - down, 1)
    scale = np.exp2(byte - 127.0)
    codes = (blocks / scale).astype(np.float32).astype(dtype).astype(np.float64)
    return np.moveaxis((codes * scale).reshape(v.shape), -1, axis)


WIDE = False


def mx_kscale(k):
    if not WIDE:
        return np.ones(k)
    levels = np.array([24, -24, 12, -12, 0])
    if k % 512:
        return np.exp2(np.random.permutation(np.resize(levels, k // 32))).repeat(32)
    a = np.empty((k // 512, 16))
    for p in range(k // 512):
        a[p, :8] = np.random.permutation(np.resize(levels, 8))
        for g in range(8):
            far = levels[np.abs(levels - a[p, g]) >= 10]
            a[p, g + 8] = far[np.random.randint(len(far))]
    return np.exp2(a.ravel()).repeat(32)


def f64(x):
    return np.asarray(x).astype(np.float64)


def striped(idx):
    return np.tile(idx.reshape(-1, 16).T, (8, 1)).astype(np.uint16)


def unstriped(offs):
    return offs[:16].T.reshape(-1).astype(np.int64)


E2M1 = np.array([0.0, 0.5, 1.0, 1.5, 2.0, 3.0, 4.0, 6.0, -0.0, -0.5, -1.0, -1.5, -2.0, -3.0, -4.0, -6.0])


def pack_weight(w, fmt):
    k, n = w.shape
    w = f64(np.asarray(w, np.float32).astype(ml_dtypes.bfloat16)).reshape(k // 32, 32, n)
    amax = np.abs(w).max(1)
    if fmt == "e4m3":
        byte = np.frexp(amax)[1] - 1 + 127 - 7
    else:
        mant, ex = np.frexp(amax / 6.0)
        byte = np.where(mant > 0.5, ex, ex - 1) + 127
    byte = np.clip(np.where(amax > 0, byte, 1), 1, 254)
    scaled = (w * np.exp2(127.0 - byte)[:, None, :]).reshape(k, n).astype(np.float32)
    by_word = np.ascontiguousarray(scaled.reshape(k // 512, 128, 4, n).transpose(0, 1, 3, 2))
    if fmt == "e4m3":
        words = by_word.astype(ml_dtypes.float8_e4m3fn).view(np.uint8)
    else:
        c = by_word.astype(ml_dtypes.float4_e2m1fn).view(np.uint8) & 0xF
        words = (c[..., 0::2] | (c[..., 1::2] << 4)).reshape(k // 512, 128, 2 * n)
    return np.ascontiguousarray(words), np.ascontiguousarray(byte.astype(np.uint8).reshape(k // 512, 16, n))


def unpack_weight(words, scales, fmt):
    g, _, n = scales.shape
    words = np.ascontiguousarray(words).reshape(g, 128, n, -1)
    if fmt == "e4m3":
        vals = words.view(ml_dtypes.float8_e4m3fn).astype(np.float64)
    else:
        nib = np.empty((g, 128, n, 4), np.uint8)
        nib[..., 0::2] = words & 0xF
        nib[..., 1::2] = words >> 4
        vals = E2M1[nib]
    vals = vals * np.repeat(np.exp2(scales.astype(np.float64) - 127.0), 8, axis=1)[..., None]
    return vals.transpose(0, 1, 3, 2).reshape(g * 512, n)


def planes(y):
    n, m = y.shape
    v = y.astype(np.float32).astype(ml_dtypes.bfloat16).astype(np.float64).reshape(n // 32, 32, m)
    top = np.abs(v).max(1)
    byte = np.clip(np.where(top > 0, np.frexp(top)[1] - 1 + 127 - 7, 1), 1, 254)
    codes = (v * np.exp2(127.0 - byte)[:, None, :]).reshape(n, m).astype(np.float32).astype(ml_dtypes.float8_e4m3fn).view(np.uint8)
    words = codes.reshape(n // 512, 128, 4, m).transpose(0, 1, 3, 2)
    return np.ascontiguousarray(words), np.ascontiguousarray(byte.astype(np.uint8).reshape(n // 512, 16, m))


def sigm(f):
    return 1.0 / (1.0 + np.exp(-np.maximum(f, -700.0)))


K, M, N, T, J = 1024, 512, 512, 2048, 1024


def setup_inputs():
    n = np.random.standard_normal
    s = mx_kscale(K)[:, None]
    s2 = mx_kscale(M)[:, None]
    h = np.tanh(n((N, T)))
    p_tab = pack_weight(h * s2, "e4m3")
    p_wz = pack_weight(n((K, N)) / np.sqrt(K) / s, "e4m3")
    p_uz = pack_weight(n((M, N)) / np.sqrt(M) / s2, "e4m3")
    p_wr = pack_weight(n((K, N)) / np.sqrt(K) / s, "e4m3")
    p_ur = pack_weight(n((M, N)) / np.sqrt(M) / s2, "e4m3")
    p_wn = pack_weight(n((K, N)) / np.sqrt(K) / s, "e4m3")
    p_un = pack_weight(n((M, N)) / np.sqrt(M) / s2, "e4m3")
    return {
        "x": (n((K, J)) * s).astype(np.float32),
        "tab_words": p_tab[0],
        "tab_scales": p_tab[1],
        "wz_words": p_wz[0],
        "wz_scales": p_wz[1],
        "uz_words": p_uz[0],
        "uz_scales": p_uz[1],
        "wr_words": p_wr[0],
        "wr_scales": p_wr[1],
        "ur_words": p_ur[0],
        "ur_scales": p_ur[1],
        "wn_words": p_wn[0],
        "wn_scales": p_wn[1],
        "un_words": p_un[0],
        "un_scales": p_un[1],
        "bz": (0.3 * n(N)).astype(np.float32),
        "br": (0.3 * n(N)).astype(np.float32),
        "bn": (0.3 * n(N)).astype(np.float32),
        "hT": (h).astype(np.float32),
        "wgo": np.tile(np.random.uniform(0.5, 2.0, J), (128, 1)).astype(np.float32),
        "offs": striped(np.random.permutation(T)[:J]),
    }


def reference(x, tab_words, tab_scales, wz_words, wz_scales, uz_words, uz_scales, wr_words, wr_scales, ur_words, ur_scales, wn_words, wn_scales, un_words, un_scales, bz, br, bn, hT, wgo, offs):
    idx = unstriped(offs)
    x_ = mxq(f64(x), 0, "e4m3")
    tab_ = unpack_weight(tab_words, tab_scales, "e4m3")[:, idx]
    wz_ = unpack_weight(wz_words, wz_scales, "e4m3")
    uz_ = unpack_weight(uz_words, uz_scales, "e4m3")
    wr_ = unpack_weight(wr_words, wr_scales, "e4m3")
    ur_ = unpack_weight(ur_words, ur_scales, "e4m3")
    wn_ = unpack_weight(wn_words, wn_scales, "e4m3")
    un_ = unpack_weight(un_words, un_scales, "e4m3")
    sz = wz_.T @ x_ + uz_.T @ tab_
    z = sigm(sz + f64(bz)[:, None])
    sr = wr_.T @ x_ + ur_.T @ tab_
    r = sigm(sr + f64(br)[:, None])
    xn = wn_.T @ x_
    hn = un_.T @ tab_
    cd = np.tanh(xn + f64(bn)[:, None] + r * hn)
    out = np.zeros((N, T))
    out[:, idx] = f64(wgo)[0] * (f64(hT)[:, idx] + z * (cd - f64(hT)[:, idx]))
    return (out,) + planes(out)

@@ -1,0 +1,321 @@
+from contextlib import ExitStack
+
+import concourse.mybir as mybir
+
+K, M, N, T, J = 1024, 512, 512, 2048, 1024
+FLOPS = 2 * 3 * (K + M) * N * J
+
+F32 = mybir.dt.float32
+BF16 = mybir.dt.bfloat16
+I32 = mybir.dt.int32
+U32 = mybir.dt.uint32
+U16 = mybir.dt.uint16
+U8 = mybir.dt.uint8
+FP8X4 = mybir.dt.float8_e4m3fn_x4
+ACT = mybir.ActivationFunctionType
+ALU = mybir.AluOpType
+
+P = 128
+PACK = 4
+HALF = 512
+QUADS = 4
+LIST_COLS = HALF // 16
+GATE_Z, GATE_R, GATE_N = 0, 1, 2
+STATE_PASS = 2
+SLICE_ORDER = (2, 1, 0, 3)
+PAIRS = (slice(1, 3), slice(0, 4, 3))
+
+
+def tile_list_tgn_gruP_kernel(
+    tc, x, tab_words, tab_scales, wz_words, wz_scales, uz_words, uz_scales, wr_words, wr_scales,
+    ur_words, ur_scales, wn_words, wn_scales, un_words, un_scales, bz, br, bn, hT, wgo, offs,
+    out_0, out_1, out_2,
+):
+    nc = tc.nc
+    w_words = (wz_words, wr_words, wn_words)
+    w_scales = (wz_scales, wr_scales, wn_scales)
+    u_words = (uz_words, ur_words, un_words)
+    u_scales = (uz_scales, ur_scales, un_scales)
+    biases = (bz, br, bn)
+    h_rows = hT.rearrange("(p t) c -> p t c", t=PACK)
+    out_rows = out_0.rearrange("(p t) c -> p t c", t=PACK)
+    out_words = out_1[0].rearrange("p c i -> p (c i)").bitcast(I32)
+    out_scales = out_2[0].bitcast(I32)
+
+    with ExitStack() as ctx:
+        keep = ctx.enter_context(tc.tile_pool(name="keep", bufs=1))
+        ring = ctx.enter_context(tc.tile_pool(name="ring", bufs=2))
+        psum = ctx.enter_context(tc.psum_pool(name="psum", bufs=2))
+
+        offsets = keep.tile([P, J // 16], U16, name="offsets")
+        scale_load = keep.tile([12, 3 * QUADS, P], I32, name="scale_load", tag="h1")
+        scale_stage = keep.tile([32, 3 * QUADS, P], I32, name="scale_stage", tag="both0")
+        tab_scale_stage = keep.tile([4, QUADS, T // 4], I32, name="tab_scale_stage", tag="h3")
+        tab_scale_plane = keep.tile([P, T], U8, name="tab_scale_plane")
+        tab_codes = keep.tile([P, T], U32, name="tab_codes")
+        weight = keep.tile([P, J], F32, name="weight")
+        pages = {t: keep.tile([P, T], F32, name=f"page{t}") for t in SLICE_ORDER[:2]}
+        bias = [keep.tile([P, PACK], F32, name=f"bias{g}") for g in range(3)]
+        neg_bz = keep.tile([P, PACK], F32, name="neg_bz")
+        raw_w = [keep.tile([P, 2, N], U32, name=f"raw_w{g}") for g in range(3)]
+        raw_u = [keep.tile([P, 1, N], U32, name=f"raw_u{g}") for g in range(3)]
+        dealt = {
+            (g, a, pair): keep.tile([P, 2, P], U32, name=f"dealt{g}_{a}_{pair}", align_bytes=64)
+            for g in range(3) for a in range(3) for pair in range(2)
+        }
+        scale_rows = keep.tile([P, 3, N], U8, name="scale_rows")
+        dealt_scales = [keep.tile([P, 3, 2, P], U8, name=f"dealt_scales{pair}", align_bytes=64) for pair in range(2)]
+        mov_codes = [[keep.tile([P, HALF], U32, name=f"mov_codes{a}_{c}", align_bytes=64) for c in range(2)] for a in range(3)]
+        mov_scales = [[keep.tile([P, HALF], U8, name=f"mov_scales{a}_{c}", align_bytes=64) for c in range(2)] for a in range(3)]
+        out_codes = [keep.tile([P, HALF], U32, name=f"out_codes{c}", align_bytes=64) for c in range(4)]
+        out_plane = keep.tile([P, T], U8, name="out_plane", align_bytes=64)
+
+        x_raw, x_bf, h, keepz, cand, gated, pre = {}, {}, {}, {}, {}, {}, {}
+        banks = {}
+
+        def list_half(c):
+            return offsets[:, c * LIST_COLS : (c + 1) * LIST_COLS]
+
+        def cols(c):
+            return slice(c * HALF, (c + 1) * HALF)
+
+        def load_x(a, c):
+            x_raw[a, c] = ring.tile([P, PACK, HALF], F32, name="x_raw")
+            rows = x[a * P * PACK : (a + 1) * P * PACK, cols(c)]
+            nc.sync.dma_start(x_raw[a, c][:], rows.rearrange("(p i) j -> p i j", i=PACK))
+
+        def load_scales(g, scales, first, count):
+            nc.sync.dma_start(
+                scale_load[4 * g : 4 * g + 4, first : first + count, :],
+                scales.rearrange("a (q r) n -> r (a q) n", r=4).bitcast(I32),
+            )
+
+        def load_words(tile, words):
+            nc.sync.dma_start(tile[:].bitcast(I32), words.rearrange("a p n i -> p a (n i)").bitcast(I32))
+
+        def load_bias(g):
+            nc.sync.dma_start(bias[g][:], biases[g].rearrange("(p t) -> p t", t=PACK))
+
+        def load_h(t):
+            h[t] = keep.tile([P, T], F32, name=f"h{t}", tag=f"h{t}")
+            nc.sync.dma_start(h[t][:], h_rows[:, t, :])
+
+        def round_x(a, c, copy):
+            x_bf[a, c] = keep.tile([P, HALF, PACK], BF16, name="x_bf", tag=f"quad{2 * c + a}", align_bytes=64)
+            copy(
+                x_bf[a, c][:].rearrange("p (c i) t -> p c t i", i=4),
+                x_raw[a, c][:].rearrange("p t (c i) -> p c t i", i=4),
+            )
+
+        def quantize_x(a, c):
+            nc.vector.quantize_mx(
+                out=mov_codes[a][c][:].bitcast(FP8X4),
+                scales=mov_scales[a][c][:],
+                in_=x_bf[a, c][:].rearrange("p j t -> p (j t)"),
+            )
+
+        def deal(g, a, pair):
+            raw = raw_u[g][:, 0, :] if a == STATE_PASS else raw_w[g][:, a, :]
+            nc.scalar.copy(
+                dealt[g, a, pair][:].rearrange("p t q -> p q t"),
+                raw.rearrange("p (q t) -> p q t", t=PACK)[:, :, PAIRS[pair]],
+            )
+
+        def deal_scales(pair):
+            nc.vector.tensor_copy(
+                dealt_scales[pair][:],
+                scale_rows[:].rearrange("p a (q t) -> p a t q", t=PACK)[:, :, PAIRS[pair], :],
+            )
+
+        def product(tag, g, passes, t, c):
+            bank = psum.tile([P, HALF], F32, name=tag, tag=tag)
+            pair = SLICE_ORDER.index(t) // 2
+            place = range(PACK)[PAIRS[pair]].index(t)
+            for a in passes:
+                nc.tensor.matmul_mx(
+                    out=bank[:],
+                    lhsT=dealt[g, a, pair][:, place, :].bitcast(FP8X4),
+                    lhsT_scale=dealt_scales[pair][4 * g : P, a, place, :],
+                    rhs=mov_codes[a][c][:].bitcast(FP8X4),
+                    rhs_scale=mov_scales[a][c][:],
+                    start=(a == passes[0]),
+                    stop=(a == passes[-1]),
+                )
+            return bank
+
+        def candidates(ts, c):
+            reset = {}
+            for t in ts:
+                sr = product("sr", GATE_R, (0, 1, 2), t, c)
+                banks["hn", t] = product("hn", GATE_N, (2,), t, c)
+                banks["xn", t] = product("xn", GATE_N, (0, 1), t, c)
+                reset[t] = ring.tile([P, HALF], F32, name="reset")
+                nc.scalar.activation(reset[t][:], sr[:], ACT.Sigmoid, bias=bias[GATE_R][:, t : t + 1])
+            for t in ts:
+                pre[t, c] = ring.tile([P, HALF], F32, name="pre", bufs=3)
+                nc.vector.tensor_tensor(pre[t, c][:], banks["hn", t][:], reset[t][:], ALU.mult)
+            for t in ts:
+                nc.vector.tensor_tensor(pre[t, c][:], banks["xn", t][:], pre[t, c][:], ALU.add)
+
+        def squash(t, c, tag):
+            cand[t, c] = keep.tile([P, HALF], F32, name="cand", tag=tag)
+            nc.scalar.activation(cand[t, c][:], pre[t, c][:], ACT.Tanh, bias=bias[GATE_N][:, t : t + 1])
+
+        def keep_gate(t, c):
+            sz = product("sz", GATE_Z, (0, 1, 2), t, c)
+            keepz[t, c] = keep.tile([P, HALF], F32, name=f"keepz{t}_{c}")
+            nc.scalar.activation(keepz[t, c][:], sz[:], ACT.Sigmoid, bias=neg_bz[:, t : t + 1], scale=-1.0)
+
+        def blend(units):
+            for t, c in units:
+                nc.vector.tensor_tensor(gated[t, c], h[t][:].indirect(list_half(c)), cand[t, c][:], ALU.subtract)
+            for t, c in units:
+                nc.vector.tensor_tensor(gated[t, c], gated[t, c], keepz[t, c][:], ALU.mult)
+            for t, c in units:
+                nc.vector.tensor_tensor(gated[t, c], gated[t, c], cand[t, c][:], ALU.add)
+
+        grouped = {}
+
+        def round_plane(t, c, copy):
+            if c not in grouped:
+                grouped[c] = keep.tile([P, HALF, PACK], BF16, name="grouped", tag=f"quad{c}", align_bytes=64)
+            copy(grouped[c][:, :, t], pages[t][:, cols(c)])
+
+        nc.vector.memset(scale_stage[:], 0)
+        nc.vector.memset(tab_scale_plane[:].bitcast(I32), 0)
+        load_x(0, 0)
+        for g in (GATE_R, GATE_N, GATE_Z):
+            load_scales(g, w_scales[g], 0, 8)
+            load_scales(g, u_scales[g], 8, 4)
+        load_x(1, 0)
+        nc.sync.dma_start(tab_scale_stage[:], tab_scales[0].rearrange("(q r) t -> r q t", r=4).bitcast(I32))
+        nc.sync.dma_start(offsets[:], offs)
+        nc.sync.dma_start(tab_codes[:].bitcast(I32), tab_words[0].rearrange("p t i -> p (t i)").bitcast(I32))
+        load_words(raw_w[GATE_R], w_words[GATE_R])
+        load_words(raw_u[GATE_R], u_words[GATE_R])
+        load_bias(GATE_R)
+        load_words(raw_u[GATE_N], u_words[GATE_N])
+        load_words(raw_w[GATE_N], w_words[GATE_N])
+        load_bias(GATE_N)
+        load_words(raw_w[GATE_Z], w_words[GATE_Z])
+        load_words(raw_u[GATE_Z], u_words[GATE_Z])
+        load_bias(GATE_Z)
+        first, second, third, last = SLICE_ORDER
+        load_h(first)
+        load_h(second)
+        nc.sync.dma_start(weight[:], wgo)
+
+        for t in (first, second):
+            nc.vector.memset(pages[t][:], 0.0)
+
+        nc.scalar.copy(scale_stage[0:12, :, :].bitcast(U32), scale_load[:].bitcast(U32))
+        rows32 = scale_rows[:].bitcast(I32)
+        nc.vector.tensor_copy(rows32[0:32, :, :], scale_stage[0:32, 0 : 3 * QUADS : QUADS, :])
+        for q in range(1, QUADS):
+            for a in range(3):
+                nc.vector.tensor_copy(rows32[32 * q : 32 * q + 32, a, :], scale_stage[0:32, QUADS * a + q, :])
+        deal_scales(0)
+
+        def gather_table(c):
+            nc.vector.tensor_copy(mov_scales[STATE_PASS][c][:], tab_scale_plane[:].indirect(list_half(c)))
+            nc.vector.tensor_copy(mov_codes[STATE_PASS][c][:], tab_codes[:].indirect(list_half(c)))
+
+        round_x(0, 0, nc.scalar.copy)
+        round_x(1, 0, nc.vector.tensor_copy)
+        for q in range(QUADS):
+            nc.vector.tensor_copy(tab_scale_plane[32 * q : 32 * q + 4, :].bitcast(I32), tab_scale_stage[:, q, :])
+        quantize_x(0, 0)
+        quantize_x(1, 0)
+        gather_table(0)
+        deal_scales(1)
+
+        load_x(0, 1)
+        load_x(1, 1)
+        load_h(third)
+        load_h(last)
+
+        for pair in range(2):
+            for g, a in ((GATE_R, 0), (GATE_R, 1), (GATE_R, 2), (GATE_N, 2), (GATE_N, 0), (GATE_N, 1)):
+                deal(g, a, pair)
+        nc.vector.tensor_scalar(neg_bz[:], bias[GATE_Z][:], -1.0, None, ALU.mult)
+
+        candidates((first, second), 0)
+        for a in range(3):
+            deal(GATE_Z, a, 0)
+        squash(first, 0, "cand_a")
+        squash(second, 0, "cand_b")
+        candidates((third, last), 0)
+        keep_gate(first, 0)
+        keep_gate(second, 0)
+        for a in range(3):
+            deal(GATE_Z, a, 1)
+        gather_table(1)
+        squash(third, 0, "cand_c")
+        squash(last, 0, "cand_d")
+        keep_gate(third, 0)
+        keep_gate(last, 0)
+        for a in range(2):
+            round_x(a, 1, nc.scalar.copy)
+        for t in (third, last):
+            pages[t] = ring.tile([P, T], F32, name="late_page", tag="x_raw")
+            nc.gpsimd.memset(pages[t][:], 0.0)
+
+        for t in (first, second):
+            for c in range(2):
+                gated[t, c] = keep.tile([P, HALF], F32, name="gated", tag=f"gated{t}_{c}")[:]
+
+        def place(t, c):
+            nc.vector.tensor_tensor(pages[t][:].indirect(list_half(c)), gated[t, c], weight[:, cols(c)], ALU.mult)
+
+        blend(((first, 0), (second, 0)))
+        place(first, 0)
+        quantize_x(0, 1)
+        quantize_x(1, 1)
+        place(second, 0)
+
+        candidates((first, second), 1)
+        squash(first, 1, "cand_a")
+        squash(second, 1, "cand_b")
+        keep_gate(first, 1)
+        keep_gate(second, 1)
+        candidates((third, last), 1)
+        squash(third, 1, "cand_e")
+        keep_gate(third, 1)
+        keep_gate(last, 1)
+
+        blend(((first, 1), (second, 1)))
+        place(first, 1)
+        nc.sync.dma_start(out_rows[:, first, :], pages[first][:])
+        for c in range(4):
+            round_plane(first, c, nc.scalar.copy)
+        squash(last, 1, f"gated{first}_1")
+        place(second, 1)
+        nc.sync.dma_start(out_rows[:, second, :], pages[second][:])
+        for c in range(4):
+            round_plane(second, c, nc.scalar.copy)
+
+        for t in (third, last):
+            both = keep.tile([P, J], F32, name="both", tag=f"both{int(t == last)}")
+            for c in range(2):
+                gated[t, c] = both[:, cols(c)]
+            blend(((t, 0), (t, 1)))
+            nc.vector.tensor_tensor(pages[t][:].indirect(offsets[:]), both[:], weight[:], ALU.mult)
+            nc.sync.dma_start(out_rows[:, t, :], pages[t][:])
+            if t == third:
+                for c in range(4):
+                    round_plane(t, c, nc.scalar.copy)
+
+        round_plane(last, 2, nc.scalar.copy)
+        round_plane(last, 3, nc.scalar.copy)
+        round_plane(last, 0, nc.vector.tensor_copy)
+        round_plane(last, 1, nc.vector.tensor_copy)
+        for c in range(4):
+            nc.vector.quantize_mx(
+                out=out_codes[c][:].bitcast(FP8X4),
+                scales=out_plane[:, cols(c)],
+                in_=grouped[c][:].rearrange("p j t -> p (j t)"),
+            )
+            nc.sync.dma_start(out_words[:, cols(c)], out_codes[c][:].bitcast(I32))
+        for q in range(QUADS):
+            queue = nc.scalar if q % 2 else nc.sync
+            queue.dma_start(out_scales[4 * q : 4 * q + 4, :], out_plane[32 * q : 32 * q + 4, :].bitcast(I32))

@@ -44,28 +44,30 @@ def tile_list_tgn_gruP_kernel(
 
     with ExitStack() as ctx:
         keep = ctx.enter_context(tc.tile_pool(name="keep", bufs=1))
-        ring = ctx.enter_context(tc.tile_pool(name="ring", bufs=2))
         psum = ctx.enter_context(tc.psum_pool(name="psum", bufs=2))
 
         offsets = keep.tile([P, J // 16], U16, name="offsets")
-        scale_load = keep.tile([12, 3 * QUADS, P], I32, name="scale_load", tag="h1")
-        scale_stage = keep.tile([32, 3 * QUADS, P], I32, name="scale_stage", tag="both0")
-        tab_scale_stage = keep.tile([4, QUADS, T // 4], I32, name="tab_scale_stage", tag="h3")
+        scale_load = keep.tile([12, 3 * QUADS, P], I32, name="scale_load", tag="quad2", align_bytes=64)
+        scale_stage = keep.tile([32, QUADS - 1, 3, P], I32, name="scale_stage", tag="keepz3_1")
+        tab_scale_stage = keep.tile([4, QUADS, T // 4], I32, name="tab_scale_stage", tag="quad3", align_bytes=64)
         tab_scale_plane = keep.tile([P, T], U8, name="tab_scale_plane")
         tab_codes = keep.tile([P, T], U32, name="tab_codes")
         weight = keep.tile([P, J], F32, name="weight")
-        pages = {t: keep.tile([P, T], F32, name=f"page{t}") for t in SLICE_ORDER[:2]}
+        pages = {t: keep.tile([P, T], F32, name="page", tag=f"page{t}") for t in SLICE_ORDER[:2]}
         bias = [keep.tile([P, PACK], F32, name=f"bias{g}") for g in range(3)]
         neg_bz = keep.tile([P, PACK], F32, name="neg_bz")
         raw_w = [keep.tile([P, 2, N], U32, name=f"raw_w{g}") for g in range(3)]
         raw_u = [keep.tile([P, 1, N], U32, name=f"raw_u{g}") for g in range(3)]
         dealt = {
             (g, a, pair): keep.tile([P, 2, P], U32, name=f"dealt{g}_{a}_{pair}", align_bytes=64)
-            for g in range(3) for a in range(3) for pair in range(2)
+            for g in (GATE_R, GATE_N) for a in range(3) for pair in range(2)
         }
         scale_rows = keep.tile([P, 3, N], U8, name="scale_rows")
         dealt_scales = [keep.tile([P, 3, 2, P], U8, name=f"dealt_scales{pair}", align_bytes=64) for pair in range(2)]
-        mov_codes = [[keep.tile([P, HALF], U32, name=f"mov_codes{a}_{c}", align_bytes=64) for c in range(2)] for a in range(3)]
+        mov_codes = {
+            (a, c): keep.tile([P, HALF], U32, name=f"mov_codes{a}_{c}", align_bytes=64)
+            for a, c in ((0, 0), (1, 0), (2, 0), (2, 1))
+        }
         mov_scales = [[keep.tile([P, HALF], U8, name=f"mov_scales{a}_{c}", align_bytes=64) for c in range(2)] for a in range(3)]
         out_codes = [keep.tile([P, HALF], U32, name=f"out_codes{c}", align_bytes=64) for c in range(4)]
         out_plane = keep.tile([P, T], U8, name="out_plane", align_bytes=64)
@@ -80,7 +82,7 @@ def tile_list_tgn_gruP_kernel(
             return slice(c * HALF, (c + 1) * HALF)
 
         def load_x(a, c):
-            x_raw[a, c] = ring.tile([P, PACK, HALF], F32, name="x_raw")
+            x_raw[a, c] = keep.tile([P, PACK, HALF], F32, name="x_raw", tag=f"x_raw{a}_{c}")
             rows = x[a * P * PACK : (a + 1) * P * PACK, cols(c)]
             nc.sync.dma_start(x_raw[a, c][:], rows.rearrange("(p i) j -> p i j", i=PACK))
 
@@ -96,20 +98,24 @@ def tile_list_tgn_gruP_kernel(
         def load_bias(g):
             nc.sync.dma_start(bias[g][:], biases[g].rearrange("(p t) -> p t", t=PACK))
 
-        def load_h(t):
-            h[t] = keep.tile([P, T], F32, name=f"h{t}", tag=f"h{t}")
+        def load_h(t, tag):
+            h[t] = keep.tile([P, T], F32, name="h", tag=tag)
             nc.sync.dma_start(h[t][:], h_rows[:, t, :])
 
-        def round_x(a, c, copy):
-            x_bf[a, c] = keep.tile([P, HALF, PACK], BF16, name="x_bf", tag=f"quad{2 * c + a}", align_bytes=64)
-            copy(
+        def round_x_scalar(a, c, tag):
+            x_bf[a, c] = keep.tile([P, HALF, PACK], BF16, name="x_bf", tag=tag, align_bytes=64)
+            nc.scalar.copy(
                 x_bf[a, c][:].rearrange("p (c i) t -> p c t i", i=4),
                 x_raw[a, c][:].rearrange("p t (c i) -> p c t i", i=4),
             )
 
+        def round_x_gpsimd(a, c, tag):
+            x_bf[a, c] = keep.tile([P, HALF, PACK], BF16, name="x_bf", tag=tag, align_bytes=64)
+            nc.gpsimd.tensor_scalar(x_bf[a, c][:], x_raw[a, c][:].rearrange("p t j -> p j t"), 1.0, 0.0, ALU.mult, ALU.add)
+
         def quantize_x(a, c):
             nc.vector.quantize_mx(
-                out=mov_codes[a][c][:].bitcast(FP8X4),
+                out=mov_codes[a, c][:].bitcast(FP8X4),
                 scales=mov_scales[a][c][:],
                 in_=x_bf[a, c][:].rearrange("p j t -> p (j t)"),
             )
@@ -117,9 +123,15 @@ def tile_list_tgn_gruP_kernel(
         def deal(g, a, pair):
             raw = raw_u[g][:, 0, :] if a == STATE_PASS else raw_w[g][:, a, :]
             nc.scalar.copy(
-                dealt[g, a, pair][:].rearrange("p t q -> p q t"),
+                dealt[g, a, pair][:, :, :].rearrange("p t q -> p q t"),
                 raw.rearrange("p (q t) -> p q t", t=PACK)[:, :, PAIRS[pair]],
             )
+
+        def deal_z(pair):
+            both = keep.tile([P, 3, 2, P], U32, name="dealt_z", tag=f"early{pair}", align_bytes=64)
+            for a in range(3):
+                dealt[GATE_Z, a, pair] = both[:, a, :, :]
+                deal(GATE_Z, a, pair)
 
         def deal_scales(pair):
             nc.vector.tensor_copy(
@@ -136,43 +148,56 @@ def tile_list_tgn_gruP_kernel(
                     out=bank[:],
                     lhsT=dealt[g, a, pair][:, place, :].bitcast(FP8X4),
                     lhsT_scale=dealt_scales[pair][4 * g : P, a, place, :],
-                    rhs=mov_codes[a][c][:].bitcast(FP8X4),
+                    rhs=mov_codes[a, c][:].bitcast(FP8X4),
                     rhs_scale=mov_scales[a][c][:],
                     start=(a == passes[0]),
                     stop=(a == passes[-1]),
                 )
             return bank
 
-        def candidates(ts, c):
+        def candidates(units, reset_tags, pre_tags):
             reset = {}
-            for t in ts:
+            for (t, c), tag in zip(units, reset_tags):
                 sr = product("sr", GATE_R, (0, 1, 2), t, c)
                 banks["hn", t] = product("hn", GATE_N, (2,), t, c)
                 banks["xn", t] = product("xn", GATE_N, (0, 1), t, c)
-                reset[t] = ring.tile([P, HALF], F32, name="reset")
+                reset[t] = keep.tile([P, HALF], F32, name="reset", tag=tag, align_bytes=64)
                 nc.scalar.activation(reset[t][:], sr[:], ACT.Sigmoid, bias=bias[GATE_R][:, t : t + 1])
-            for t in ts:
-                pre[t, c] = ring.tile([P, HALF], F32, name="pre", bufs=3)
+            for (t, c), tag in zip(units, pre_tags):
+                pre[t, c] = keep.tile([P, HALF], F32, name="pre", tag=tag, align_bytes=64)
                 nc.vector.tensor_tensor(pre[t, c][:], banks["hn", t][:], reset[t][:], ALU.mult)
-            for t in ts:
+            for t, c in units:
                 nc.vector.tensor_tensor(pre[t, c][:], banks["xn", t][:], pre[t, c][:], ALU.add)
 
         def squash(t, c, tag):
-            cand[t, c] = keep.tile([P, HALF], F32, name="cand", tag=tag)
+            cand[t, c] = keep.tile([P, HALF], F32, name="cand", tag=tag, align_bytes=64)
             nc.scalar.activation(cand[t, c][:], pre[t, c][:], ACT.Tanh, bias=bias[GATE_N][:, t : t + 1])
 
         def keep_gate(t, c):
             sz = product("sz", GATE_Z, (0, 1, 2), t, c)
-            keepz[t, c] = keep.tile([P, HALF], F32, name=f"keepz{t}_{c}")
+            keepz[t, c] = keep.tile([P, HALF], F32, name="keepz", tag=f"keepz{t}_{c}")
             nc.scalar.activation(keepz[t, c][:], sz[:], ACT.Sigmoid, bias=neg_bz[:, t : t + 1], scale=-1.0)
 
-        def blend(units):
-            for t, c in units:
-                nc.vector.tensor_tensor(gated[t, c], h[t][:].indirect(list_half(c)), cand[t, c][:], ALU.subtract)
-            for t, c in units:
-                nc.vector.tensor_tensor(gated[t, c], gated[t, c], keepz[t, c][:], ALU.mult)
-            for t, c in units:
-                nc.vector.tensor_tensor(gated[t, c], gated[t, c], cand[t, c][:], ALU.add)
+        def blend(t, c, weigh=True):
+            g = keep.tile([P, HALF], F32, name="gated", tag=f"gated{len(gated) % 2}", align_bytes=64)
+            gated[t, c] = g
+            nc.vector.tensor_tensor(g[:], h[t][:].indirect(list_half(c)), cand[t, c][:], ALU.subtract)
+            nc.gpsimd.tensor_tensor(g[:], g[:], keepz[t, c][:], ALU.mult)
+            nc.gpsimd.tensor_tensor(g[:], g[:], cand[t, c][:], ALU.add)
+            if weigh:
+                nc.gpsimd.tensor_tensor(g[:], g[:], weight[:, cols(c)], ALU.mult)
+
+        def place(t, c):
+            nc.vector.tensor_copy(pages[t][:].indirect(list_half(c)), gated[t, c][:])
+
+        def clear_late_page(t, tag):
+            pages[t] = keep.tile([P, T], F32, name="late_page", tag=tag)
+            nc.gpsimd.memset(pages[t][:], 0.0)
+
+        def finish_page(t):
+            nc.sync.dma_start(out_rows[:, t, :], pages[t][:])
+            for c in range(4):
+                round_plane(t, c, nc.scalar.copy)
 
         grouped = {}
 
@@ -181,129 +206,127 @@ def tile_list_tgn_gruP_kernel(
                 grouped[c] = keep.tile([P, HALF, PACK], BF16, name="grouped", tag=f"quad{c}", align_bytes=64)
             copy(grouped[c][:, :, t], pages[t][:, cols(c)])
 
-        nc.vector.memset(scale_stage[:], 0)
         nc.vector.memset(tab_scale_plane[:].bitcast(I32), 0)
-        load_x(0, 0)
+        nc.vector.memset(scale_rows[0:32, :, :].bitcast(I32), 0)
+        nc.vector.memset(scale_stage[:], 0)
+        nc.sync.dma_start(tab_scale_stage[:], tab_scales[0].rearrange("(q r) t -> r q t", r=4).bitcast(I32))
         for g in (GATE_R, GATE_N, GATE_Z):
             load_scales(g, w_scales[g], 0, 8)
             load_scales(g, u_scales[g], 8, 4)
+        load_x(0, 0)
         load_x(1, 0)
-        nc.sync.dma_start(tab_scale_stage[:], tab_scales[0].rearrange("(q r) t -> r q t", r=4).bitcast(I32))
         nc.sync.dma_start(offsets[:], offs)
         nc.sync.dma_start(tab_codes[:].bitcast(I32), tab_words[0].rearrange("p t i -> p (t i)").bitcast(I32))
         load_words(raw_w[GATE_R], w_words[GATE_R])
         load_words(raw_u[GATE_R], u_words[GATE_R])
         load_bias(GATE_R)
+        load_bias(GATE_Z)
         load_words(raw_u[GATE_N], u_words[GATE_N])
         load_words(raw_w[GATE_N], w_words[GATE_N])
         load_bias(GATE_N)
+        load_x(0, 1)
+        load_x(1, 1)
         load_words(raw_w[GATE_Z], w_words[GATE_Z])
         load_words(raw_u[GATE_Z], u_words[GATE_Z])
-        load_bias(GATE_Z)
         first, second, third, last = SLICE_ORDER
-        load_h(first)
-        load_h(second)
+        load_h(first, "h_first")
         nc.sync.dma_start(weight[:], wgo)
+        load_h(second, "h_second")
 
-        for t in (first, second):
-            nc.vector.memset(pages[t][:], 0.0)
+        nc.vector.memset(pages[first][:], 0.0)
+        for q in range(QUADS):
+            nc.vector.tensor_copy(tab_scale_plane[32 * q : 32 * q + 4, :].bitcast(I32), tab_scale_stage[:, q, :])
 
-        nc.scalar.copy(scale_stage[0:12, :, :].bitcast(U32), scale_load[:].bitcast(U32))
-        rows32 = scale_rows[:].bitcast(I32)
-        nc.vector.tensor_copy(rows32[0:32, :, :], scale_stage[0:32, 0 : 3 * QUADS : QUADS, :])
+        by_quadrant = scale_load[:].bitcast(U32).rearrange("p (a q) n -> p q a n", q=QUADS)
+        nc.scalar.copy(scale_stage[0:12, :, :, :].bitcast(U32), by_quadrant[:, 1:QUADS, :, :])
+        nc.scalar.copy(scale_rows[0:12, :, :].bitcast(U32), by_quadrant[:, 0, :, :])
         for q in range(1, QUADS):
-            for a in range(3):
-                nc.vector.tensor_copy(rows32[32 * q : 32 * q + 32, a, :], scale_stage[0:32, QUADS * a + q, :])
+            nc.vector.tensor_copy(scale_rows[32 * q : 32 * q + 32, :, :].bitcast(I32), scale_stage[:, q - 1, :, :])
         deal_scales(0)
+        deal_scales(1)
+        nc.vector.memset(pages[second][:], 0.0)
 
         def gather_table(c):
             nc.vector.tensor_copy(mov_scales[STATE_PASS][c][:], tab_scale_plane[:].indirect(list_half(c)))
-            nc.vector.tensor_copy(mov_codes[STATE_PASS][c][:], tab_codes[:].indirect(list_half(c)))
+            nc.vector.tensor_copy(mov_codes[STATE_PASS, c][:], tab_codes[:].indirect(list_half(c)))
 
-        round_x(0, 0, nc.scalar.copy)
-        round_x(1, 0, nc.vector.tensor_copy)
-        for q in range(QUADS):
-            nc.vector.tensor_copy(tab_scale_plane[32 * q : 32 * q + 4, :].bitcast(I32), tab_scale_stage[:, q, :])
+        round_x_scalar(0, 0, "quad0")
+        round_x_scalar(1, 0, "quad1")
         quantize_x(0, 0)
         quantize_x(1, 0)
         gather_table(0)
-        deal_scales(1)
 
-        load_x(0, 1)
-        load_x(1, 1)
-        load_h(third)
-        load_h(last)
+        load_h(third, "x_raw0_0")
+        load_h(last, "x_raw1_0")
+        round_x_gpsimd(0, 1, "gated1")
+        round_x_gpsimd(1, 1, "gated0")
 
-        for pair in range(2):
+        def deal_pair(pair):
             for g, a in ((GATE_R, 0), (GATE_R, 1), (GATE_R, 2), (GATE_N, 2), (GATE_N, 0), (GATE_N, 1)):
                 deal(g, a, pair)
-        nc.vector.tensor_scalar(neg_bz[:], bias[GATE_Z][:], -1.0, None, ALU.mult)
 
-        candidates((first, second), 0)
-        for a in range(3):
-            deal(GATE_Z, a, 0)
+        deal_pair(0)
+        nc.gpsimd.tensor_scalar(neg_bz[:], bias[GATE_Z][:], -1.0, 0.0, ALU.mult, ALU.add)
+
+        candidates(((first, 0), (second, 0)), ("early0", "early1"), ("pre0", "pre1"))
+        deal_pair(1)
         squash(first, 0, "cand_a")
         squash(second, 0, "cand_b")
-        candidates((third, last), 0)
-        keep_gate(first, 0)
-        keep_gate(second, 0)
-        for a in range(3):
-            deal(GATE_Z, a, 1)
         gather_table(1)
-        squash(third, 0, "cand_c")
-        squash(last, 0, "cand_d")
-        keep_gate(third, 0)
-        keep_gate(last, 0)
+        candidates(((third, 0),), ("late_codes0",), ("late_codes1",))
+        deal_z(0)
+        squash(third, 0, "cand_e")
+        keep_gate(first, 0)
         for a in range(2):
-            round_x(a, 1, nc.scalar.copy)
-        for t in (third, last):
-            pages[t] = ring.tile([P, T], F32, name="late_page", tag="x_raw")
-            nc.gpsimd.memset(pages[t][:], 0.0)
+            mov_codes[a, 1] = keep.tile([P, HALF], U32, name="late_codes", tag=f"late_codes{a}", align_bytes=64)
+            quantize_x(a, 1)
 
-        for t in (first, second):
-            for c in range(2):
-                gated[t, c] = keep.tile([P, HALF], F32, name="gated", tag=f"gated{t}_{c}")[:]
-
-        def place(t, c):
-            nc.vector.tensor_tensor(pages[t][:].indirect(list_half(c)), gated[t, c], weight[:, cols(c)], ALU.mult)
-
-        blend(((first, 0), (second, 0)))
-        place(first, 0)
-        quantize_x(0, 1)
-        quantize_x(1, 1)
-        place(second, 0)
-
-        candidates((first, second), 1)
-        squash(first, 1, "cand_a")
-        squash(second, 1, "cand_b")
+        blend(first, 0)
+        keep_gate(second, 0)
+        blend(second, 0)
+        candidates(((first, 1),), ("reset0",), ("pre1",))
+        squash(first, 1, "cand_c")
+        candidates(((second, 1),), ("reset1",), ("pre0",))
+        squash(second, 1, "cand_d")
         keep_gate(first, 1)
         keep_gate(second, 1)
-        candidates((third, last), 1)
-        squash(third, 1, "cand_e")
-        keep_gate(third, 1)
-        keep_gate(last, 1)
-
-        blend(((first, 1), (second, 1)))
-        place(first, 1)
-        nc.sync.dma_start(out_rows[:, first, :], pages[first][:])
-        for c in range(4):
-            round_plane(first, c, nc.scalar.copy)
-        squash(last, 1, f"gated{first}_1")
-        place(second, 1)
-        nc.sync.dma_start(out_rows[:, second, :], pages[second][:])
-        for c in range(4):
-            round_plane(second, c, nc.scalar.copy)
-
+        deal_z(1)
         for t in (third, last):
-            both = keep.tile([P, J], F32, name="both", tag=f"both{int(t == last)}")
             for c in range(2):
-                gated[t, c] = both[:, cols(c)]
-            blend(((t, 0), (t, 1)))
-            nc.vector.tensor_tensor(pages[t][:].indirect(offsets[:]), both[:], weight[:], ALU.mult)
-            nc.sync.dma_start(out_rows[:, t, :], pages[t][:])
-            if t == third:
-                for c in range(4):
-                    round_plane(t, c, nc.scalar.copy)
+                keep_gate(t, c)
+
+        candidates(((third, 1),), ("reset0",), ("cand_b",))
+        squash(third, 1, "cand_a")
+        place(first, 0)
+
+        blend(first, 1)
+        clear_late_page(third, "h_first")
+        candidates(((last, 0),), ("reset1",), ("cand_c",))
+        squash(last, 0, "cand_f")
+        place(second, 0)
+
+        blend(second, 1)
+        candidates(((last, 1),), ("reset0",), ("cand_d",))
+        squash(last, 1, "cand_g")
+        place(first, 1)
+        finish_page(first)
+
+        blend(third, 0)
+        place(second, 1)
+        finish_page(second)
+
+        blend(third, 1)
+        clear_late_page(last, f"page{first}")
+        place(third, 0)
+
+        blend(last, 0)
+        place(third, 1)
+        finish_page(third)
+
+        blend(last, 1, weigh=False)
+        place(last, 0)
+        nc.vector.tensor_tensor(pages[last][:].indirect(list_half(1)), gated[last, 1][:], weight[:, cols(1)], ALU.mult)
+        nc.sync.dma_start(out_rows[:, last, :], pages[last][:])
 
         round_plane(last, 2, nc.scalar.copy)
         round_plane(last, 3, nc.scalar.copy)

@@ -53,7 +53,7 @@ def tile_list_tgn_gruP_kernel(
         tab_scale_plane = keep.tile([P, T], U8, name="tab_scale_plane")
         tab_codes = keep.tile([P, T], U32, name="tab_codes")
         weight = keep.tile([P, J], F32, name="weight")
-        pages = {t: keep.tile([P, T], F32, name="page", tag=f"page{t}") for t in SLICE_ORDER[:2]}
+        pages = {t: keep.tile([P, T], F32, name="page", tag=f"page{t}", align_bytes=64) for t in SLICE_ORDER}
         bias = [keep.tile([P, PACK], F32, name=f"bias{g}") for g in range(3)]
         neg_bz = keep.tile([P, PACK], F32, name="neg_bz")
         raw_w = [keep.tile([P, 2, N], U32, name=f"raw_w{g}") for g in range(3)]
@@ -190,10 +190,6 @@ def tile_list_tgn_gruP_kernel(
         def place(t, c):
             nc.vector.tensor_copy(pages[t][:].indirect(list_half(c)), gated[t, c][:])
 
-        def clear_late_page(t, tag):
-            pages[t] = keep.tile([P, T], F32, name="late_page", tag=tag)
-            nc.gpsimd.memset(pages[t][:], 0.0)
-
         def finish_page(t):
             nc.sync.dma_start(out_rows[:, t, :], pages[t][:])
             for c in range(4):
@@ -230,8 +226,8 @@ def tile_list_tgn_gruP_kernel(
         load_words(raw_u[GATE_Z], u_words[GATE_Z])
         first, second, third, last = SLICE_ORDER
         load_h(first, "h_first")
-        nc.sync.dma_start(weight[:], wgo)
         load_h(second, "h_second")
+        nc.sync.dma_start(weight[:], wgo)
 
         nc.vector.memset(pages[first][:], 0.0)
         for q in range(QUADS):
@@ -244,7 +240,8 @@ def tile_list_tgn_gruP_kernel(
             nc.vector.tensor_copy(scale_rows[32 * q : 32 * q + 32, :, :].bitcast(I32), scale_stage[:, q - 1, :, :])
         deal_scales(0)
         deal_scales(1)
-        nc.vector.memset(pages[second][:], 0.0)
+        for t in (second, third, last):
+            nc.vector.memset(pages[t][:], 0.0)
 
         def gather_table(c):
             nc.vector.tensor_copy(mov_scales[STATE_PASS][c][:], tab_scale_plane[:].indirect(list_half(c)))
@@ -300,23 +297,21 @@ def tile_list_tgn_gruP_kernel(
         place(first, 0)
 
         blend(first, 1)
-        clear_late_page(third, "h_first")
         candidates(((last, 0),), ("reset1",), ("cand_c",))
         squash(last, 0, "cand_f")
         place(second, 0)
 
         blend(second, 1)
         candidates(((last, 1),), ("reset0",), ("cand_d",))
-        squash(last, 1, "cand_g")
         place(first, 1)
         finish_page(first)
+        squash(last, 1, f"page{first}")
 
         blend(third, 0)
         place(second, 1)
         finish_page(second)
 
         blend(third, 1)
-        clear_late_page(last, f"page{first}")
         place(third, 0)
 
         blend(last, 0)

from contextlib import ExitStack

import concourse.mybir as mybir

K, M, N, T, J = 1024, 512, 512, 2048, 1024
FLOPS = 2 * 3 * (K + M) * N * J

F32 = mybir.dt.float32
BF16 = mybir.dt.bfloat16
I32 = mybir.dt.int32
U32 = mybir.dt.uint32
U16 = mybir.dt.uint16
U8 = mybir.dt.uint8
FP8X4 = mybir.dt.float8_e4m3fn_x4
ACT = mybir.ActivationFunctionType
ALU = mybir.AluOpType

P = 128
PACK = 4
HALF = 512
QUADS = 4
LIST_COLS = HALF // 16
GATE_Z, GATE_R, GATE_N = 0, 1, 2
STATE_PASS = 2
SLICE_ORDER = (2, 1, 0, 3)
PAIRS = (slice(1, 3), slice(0, 4, 3))


def tile_list_tgn_gruP_kernel(
    tc, x, tab_words, tab_scales, wz_words, wz_scales, uz_words, uz_scales, wr_words, wr_scales,
    ur_words, ur_scales, wn_words, wn_scales, un_words, un_scales, bz, br, bn, hT, wgo, offs,
    out_0, out_1, out_2,
):
    nc = tc.nc
    w_words = (wz_words, wr_words, wn_words)
    w_scales = (wz_scales, wr_scales, wn_scales)
    u_words = (uz_words, ur_words, un_words)
    u_scales = (uz_scales, ur_scales, un_scales)
    biases = (bz, br, bn)
    h_rows = hT.rearrange("(p t) c -> p t c", t=PACK)
    out_rows = out_0.rearrange("(p t) c -> p t c", t=PACK)
    out_words = out_1[0].rearrange("p c i -> p (c i)").bitcast(I32)
    out_scales = out_2[0].bitcast(I32)

    with ExitStack() as ctx:
        keep = ctx.enter_context(tc.tile_pool(name="keep", bufs=1))
        psum = ctx.enter_context(tc.psum_pool(name="psum", bufs=2))

        offsets = keep.tile([P, J // 16], U16, name="offsets")
        scale_load = keep.tile([12, 3 * QUADS, P], I32, name="scale_load", tag="quad2", align_bytes=64)
        scale_stage = keep.tile([32, QUADS - 1, 3, P], I32, name="scale_stage", tag="keepz3_1")
        tab_scale_stage = keep.tile([4, QUADS, T // 4], I32, name="tab_scale_stage", tag="quad3", align_bytes=64)
        tab_scale_plane = keep.tile([P, T], U8, name="tab_scale_plane")
        tab_codes = keep.tile([P, T], U32, name="tab_codes")
        weight = keep.tile([P, J], F32, name="weight")
        pages = {t: keep.tile([P, T], F32, name="page", tag=f"page{t}", align_bytes=64) for t in SLICE_ORDER}
        bias = [keep.tile([P, PACK], F32, name=f"bias{g}") for g in range(3)]
        neg_bz = keep.tile([P, PACK], F32, name="neg_bz")
        raw_w = [keep.tile([P, 2, N], U32, name=f"raw_w{g}") for g in range(3)]
        raw_u = [keep.tile([P, 1, N], U32, name=f"raw_u{g}") for g in range(3)]
        dealt = {
            (g, a, pair): keep.tile([P, 2, P], U32, name=f"dealt{g}_{a}_{pair}", align_bytes=64)
            for g in (GATE_R, GATE_N) for a in range(3) for pair in range(2)
        }
        scale_rows = keep.tile([P, 3, N], U8, name="scale_rows")
        dealt_scales = [keep.tile([P, 3, 2, P], U8, name=f"dealt_scales{pair}", align_bytes=64) for pair in range(2)]
        mov_codes = {
            (a, c): keep.tile([P, HALF], U32, name=f"mov_codes{a}_{c}", align_bytes=64)
            for a, c in ((0, 0), (1, 0), (2, 0), (2, 1))
        }
        mov_scales = [[keep.tile([P, HALF], U8, name=f"mov_scales{a}_{c}", align_bytes=64) for c in range(2)] for a in range(3)]
        out_codes = [keep.tile([P, HALF], U32, name=f"out_codes{c}", align_bytes=64) for c in range(4)]
        out_plane = keep.tile([P, T], U8, name="out_plane", align_bytes=64)

        x_raw, x_bf, h, keepz, cand, gated, pre = {}, {}, {}, {}, {}, {}, {}
        banks = {}

        def list_half(c):
            return offsets[:, c * LIST_COLS : (c + 1) * LIST_COLS]

        def cols(c):
            return slice(c * HALF, (c + 1) * HALF)

        def load_x(a, c):
            x_raw[a, c] = keep.tile([P, PACK, HALF], F32, name="x_raw", tag=f"x_raw{a}_{c}")
            rows = x[a * P * PACK : (a + 1) * P * PACK, cols(c)]
            nc.sync.dma_start(x_raw[a, c][:], rows.rearrange("(p i) j -> p i j", i=PACK))

        def load_scales(g, scales, first, count):
            nc.sync.dma_start(
                scale_load[4 * g : 4 * g + 4, first : first + count, :],
                scales.rearrange("a (q r) n -> r (a q) n", r=4).bitcast(I32),
            )

        def load_words(tile, words):
            nc.sync.dma_start(tile[:].bitcast(I32), words.rearrange("a p n i -> p a (n i)").bitcast(I32))

        def load_bias(g):
            nc.sync.dma_start(bias[g][:], biases[g].rearrange("(p t) -> p t", t=PACK))

        def load_h(t, tag):
            h[t] = keep.tile([P, T], F32, name="h", tag=tag)
            nc.sync.dma_start(h[t][:], h_rows[:, t, :])

        def round_x_scalar(a, c, tag):
            x_bf[a, c] = keep.tile([P, HALF, PACK], BF16, name="x_bf", tag=tag, align_bytes=64)
            nc.scalar.copy(
                x_bf[a, c][:].rearrange("p (c i) t -> p c t i", i=4),
                x_raw[a, c][:].rearrange("p t (c i) -> p c t i", i=4),
            )

        def round_x_gpsimd(a, c, tag):
            x_bf[a, c] = keep.tile([P, HALF, PACK], BF16, name="x_bf", tag=tag, align_bytes=64)
            nc.gpsimd.tensor_scalar(x_bf[a, c][:], x_raw[a, c][:].rearrange("p t j -> p j t"), 1.0, 0.0, ALU.mult, ALU.add)

        def quantize_x(a, c):
            nc.vector.quantize_mx(
                out=mov_codes[a, c][:].bitcast(FP8X4),
                scales=mov_scales[a][c][:],
                in_=x_bf[a, c][:].rearrange("p j t -> p (j t)"),
            )

        def deal(g, a, pair):
            raw = raw_u[g][:, 0, :] if a == STATE_PASS else raw_w[g][:, a, :]
            nc.scalar.copy(
                dealt[g, a, pair][:, :, :].rearrange("p t q -> p q t"),
                raw.rearrange("p (q t) -> p q t", t=PACK)[:, :, PAIRS[pair]],
            )

        def deal_z(pair):
            both = keep.tile([P, 3, 2, P], U32, name="dealt_z", tag=f"early{pair}", align_bytes=64)
            for a in range(3):
                dealt[GATE_Z, a, pair] = both[:, a, :, :]
                deal(GATE_Z, a, pair)

        def deal_scales(pair):
            nc.vector.tensor_copy(
                dealt_scales[pair][:],
                scale_rows[:].rearrange("p a (q t) -> p a t q", t=PACK)[:, :, PAIRS[pair], :],
            )

        def product(tag, g, passes, t, c):
            bank = psum.tile([P, HALF], F32, name=tag, tag=tag)
            pair = SLICE_ORDER.index(t) // 2
            place = range(PACK)[PAIRS[pair]].index(t)
            for a in passes:
                nc.tensor.matmul_mx(
                    out=bank[:],
                    lhsT=dealt[g, a, pair][:, place, :].bitcast(FP8X4),
                    lhsT_scale=dealt_scales[pair][4 * g : P, a, place, :],
                    rhs=mov_codes[a, c][:].bitcast(FP8X4),
                    rhs_scale=mov_scales[a][c][:],
                    start=(a == passes[0]),
                    stop=(a == passes[-1]),
                )
            return bank

        def candidates(units, reset_tags, pre_tags):
            reset = {}
            for (t, c), tag in zip(units, reset_tags):
                sr = product("sr", GATE_R, (0, 1, 2), t, c)
                banks["hn", t] = product("hn", GATE_N, (2,), t, c)
                banks["xn", t] = product("xn", GATE_N, (0, 1), t, c)
                reset[t] = keep.tile([P, HALF], F32, name="reset", tag=tag, align_bytes=64)
                nc.scalar.activation(reset[t][:], sr[:], ACT.Sigmoid, bias=bias[GATE_R][:, t : t + 1])
            for (t, c), tag in zip(units, pre_tags):
                pre[t, c] = keep.tile([P, HALF], F32, name="pre", tag=tag, align_bytes=64)
                nc.vector.tensor_tensor(pre[t, c][:], banks["hn", t][:], reset[t][:], ALU.mult)
            for t, c in units:
                nc.vector.tensor_tensor(pre[t, c][:], banks["xn", t][:], pre[t, c][:], ALU.add)

        def squash(t, c, tag):
            cand[t, c] = keep.tile([P, HALF], F32, name="cand", tag=tag, align_bytes=64)
            nc.scalar.activation(cand[t, c][:], pre[t, c][:], ACT.Tanh, bias=bias[GATE_N][:, t : t + 1])

        def keep_gate(t, c):
            sz = product("sz", GATE_Z, (0, 1, 2), t, c)
            keepz[t, c] = keep.tile([P, HALF], F32, name="keepz", tag=f"keepz{t}_{c}")
            nc.scalar.activation(keepz[t, c][:], sz[:], ACT.Sigmoid, bias=neg_bz[:, t : t + 1], scale=-1.0)

        def blend(t, c, weigh=True):
            g = keep.tile([P, HALF], F32, name="gated", tag=f"gated{len(gated) % 2}", align_bytes=64)
            gated[t, c] = g
            nc.vector.tensor_tensor(g[:], h[t][:].indirect(list_half(c)), cand[t, c][:], ALU.subtract)
            nc.gpsimd.tensor_tensor(g[:], g[:], keepz[t, c][:], ALU.mult)
            nc.gpsimd.tensor_tensor(g[:], g[:], cand[t, c][:], ALU.add)
            if weigh:
                nc.gpsimd.tensor_tensor(g[:], g[:], weight[:, cols(c)], ALU.mult)

        def place(t, c):
            nc.vector.tensor_copy(pages[t][:].indirect(list_half(c)), gated[t, c][:])

        def finish_page(t):
            nc.sync.dma_start(out_rows[:, t, :], pages[t][:])
            for c in range(4):
                round_plane(t, c, nc.scalar.copy)

        grouped = {}

        def round_plane(t, c, copy):
            if c not in grouped:
                grouped[c] = keep.tile([P, HALF, PACK], BF16, name="grouped", tag=f"quad{c}", align_bytes=64)
            copy(grouped[c][:, :, t], pages[t][:, cols(c)])

        nc.vector.memset(tab_scale_plane[:].bitcast(I32), 0)
        nc.vector.memset(scale_rows[0:32, :, :].bitcast(I32), 0)
        nc.vector.memset(scale_stage[:], 0)
        nc.sync.dma_start(tab_scale_stage[:], tab_scales[0].rearrange("(q r) t -> r q t", r=4).bitcast(I32))
        for g in (GATE_R, GATE_N, GATE_Z):
            load_scales(g, w_scales[g], 0, 8)
            load_scales(g, u_scales[g], 8, 4)
        load_x(0, 0)
        load_x(1, 0)
        nc.sync.dma_start(offsets[:], offs)
        nc.sync.dma_start(tab_codes[:].bitcast(I32), tab_words[0].rearrange("p t i -> p (t i)").bitcast(I32))
        load_words(raw_w[GATE_R], w_words[GATE_R])
        load_words(raw_u[GATE_R], u_words[GATE_R])
        load_bias(GATE_R)
        load_bias(GATE_Z)
        load_words(raw_u[GATE_N], u_words[GATE_N])
        load_words(raw_w[GATE_N], w_words[GATE_N])
        load_bias(GATE_N)
        load_x(0, 1)
        load_x(1, 1)
        load_words(raw_w[GATE_Z], w_words[GATE_Z])
        load_words(raw_u[GATE_Z], u_words[GATE_Z])
        first, second, third, last = SLICE_ORDER
        load_h(first, "h_first")
        load_h(second, "h_second")
        nc.sync.dma_start(weight[:], wgo)

        nc.vector.memset(pages[first][:], 0.0)
        for q in range(QUADS):
            nc.vector.tensor_copy(tab_scale_plane[32 * q : 32 * q + 4, :].bitcast(I32), tab_scale_stage[:, q, :])

        by_quadrant = scale_load[:].bitcast(U32).rearrange("p (a q) n -> p q a n", q=QUADS)
        nc.scalar.copy(scale_stage[0:12, :, :, :].bitcast(U32), by_quadrant[:, 1:QUADS, :, :])
        nc.scalar.copy(scale_rows[0:12, :, :].bitcast(U32), by_quadrant[:, 0, :, :])
        for q in range(1, QUADS):
            nc.vector.tensor_copy(scale_rows[32 * q : 32 * q + 32, :, :].bitcast(I32), scale_stage[:, q - 1, :, :])
        deal_scales(0)
        deal_scales(1)
        for t in (second, third, last):
            nc.vector.memset(pages[t][:], 0.0)

        def gather_table(c):
            nc.vector.tensor_copy(mov_scales[STATE_PASS][c][:], tab_scale_plane[:].indirect(list_half(c)))
            nc.vector.tensor_copy(mov_codes[STATE_PASS, c][:], tab_codes[:].indirect(list_half(c)))

        round_x_scalar(0, 0, "quad0")
        round_x_scalar(1, 0, "quad1")
        quantize_x(0, 0)
        quantize_x(1, 0)
        gather_table(0)

        load_h(third, "x_raw0_0")
        load_h(last, "x_raw1_0")
        round_x_gpsimd(0, 1, "gated1")
        round_x_gpsimd(1, 1, "gated0")

        def deal_pair(pair):
            for g, a in ((GATE_R, 0), (GATE_R, 1), (GATE_R, 2), (GATE_N, 2), (GATE_N, 0), (GATE_N, 1)):
                deal(g, a, pair)

        deal_pair(0)
        nc.gpsimd.tensor_scalar(neg_bz[:], bias[GATE_Z][:], -1.0, 0.0, ALU.mult, ALU.add)

        candidates(((first, 0), (second, 0)), ("early0", "early1"), ("pre0", "pre1"))
        deal_pair(1)
        squash(first, 0, "cand_a")
        squash(second, 0, "cand_b")
        gather_table(1)
        candidates(((third, 0),), ("late_codes0",), ("late_codes1",))
        deal_z(0)
        squash(third, 0, "cand_e")
        keep_gate(first, 0)
        for a in range(2):
            mov_codes[a, 1] = keep.tile([P, HALF], U32, name="late_codes", tag=f"late_codes{a}", align_bytes=64)
            quantize_x(a, 1)

        blend(first, 0)
        keep_gate(second, 0)
        blend(second, 0)
        candidates(((first, 1),), ("reset0",), ("pre1",))
        squash(first, 1, "cand_c")
        candidates(((second, 1),), ("reset1",), ("pre0",))
        squash(second, 1, "cand_d")
        keep_gate(first, 1)
        keep_gate(second, 1)
        deal_z(1)
        for t in (third, last):
            for c in range(2):
                keep_gate(t, c)

        candidates(((third, 1),), ("reset0",), ("cand_b",))
        squash(third, 1, "cand_a")
        place(first, 0)

        blend(first, 1)
        candidates(((last, 0),), ("reset1",), ("cand_c",))
        squash(last, 0, "cand_f")
        place(second, 0)

        blend(second, 1)
        candidates(((last, 1),), ("reset0",), ("cand_d",))
        place(first, 1)
        finish_page(first)
        squash(last, 1, f"page{first}")

        blend(third, 0)
        place(second, 1)
        finish_page(second)

        blend(third, 1)
        place(third, 0)

        blend(last, 0)
        place(third, 1)
        finish_page(third)

        blend(last, 1, weigh=False)
        place(last, 0)
        nc.vector.tensor_tensor(pages[last][:].indirect(list_half(1)), gated[last, 1][:], weight[:, cols(1)], ALU.mult)
        nc.sync.dma_start(out_rows[:, last, :], pages[last][:])

        round_plane(last, 2, nc.scalar.copy)
        round_plane(last, 3, nc.scalar.copy)
        round_plane(last, 0, nc.vector.tensor_copy)
        round_plane(last, 1, nc.vector.tensor_copy)
        for c in range(4):
            nc.vector.quantize_mx(
                out=out_codes[c][:].bitcast(FP8X4),
                scales=out_plane[:, cols(c)],
                in_=grouped[c][:].rearrange("p j t -> p (j t)"),
            )
            nc.sync.dma_start(out_words[:, cols(c)], out_codes[c][:].bitcast(I32))
        for q in range(QUADS):
            queue = nc.scalar if q % 2 else nc.sync
            queue.dma_start(out_scales[4 * q : 4 * q + 4, :], out_plane[32 * q : 32 * q + 4, :].bitcast(I32))
